import numpy as np, ml_dtypes
CORES = [100,101,102,103,108,109,110,111]
N = 8
import mx_ref
NC, G = 128, 2
C, C2 = np.float32(0.041), np.float32(0.0145)
BF = ml_dtypes.bfloat16
def cut(t, i, w=512):
    return t[:, w * i:w * i + w]
def tile(rs):
    return np.stack(rs, axis=2).reshape(128, -1).astype(BF)
def layer(w, X):
    out = []
    for i in range(G):
        for t in range(len(X)):
            p = mx_ref.matmul(mx_ref.quantize(cut(w, len(X) * i + t)), X[t])
            z = p if t == 0 else z + p
        out.append(z)
    return out
def act(Z):
    return [np.maximum(s * z, 0) * C for z in Z for s in (1, -1)]
def act2(Z):
    return [np.maximum(s * z, 0) * C2 for z in Z for s in (1, -1)]
def setup_inputs(rng):
    def f(*shape):
        return mx_ref.flush((rng.standard_normal(shape, dtype=np.float32) * np.exp2(rng.integers(-2, 3, shape[:-1] + (1,)))).astype(BF))
    return {"x": f(N, 128, 4 * NC), "w1": f(N, 128, G * 512), "w2": f(N, 128, G * 512), "w3": f(N, 128, G * 512)}
def setup_inputs_blocks(rng):
    d = setup_inputs(rng)
    for k in ("x", "w1", "w2", "w3"): d[k] = mx_ref.spread(d[k], rng, 2)
    return d
def setup_inputs_wide(rng):
    d = setup_inputs(rng)
    for k in ("x", "w1", "w2", "w3"): d[k] = mx_ref.flush((d[k].astype(np.float32) * np.exp2(rng.integers(-4, 5, (N, 1, 1))).astype(np.float32)).astype(BF))
    return d
def reference(x, w1, w2, w3, own=None):
    X = [mx_ref.quantize(x[j]) for j in range(N)]
    t = np.stack([np.stack([tile(act(layer(w1[r], [X[c]]))) for c in range(N)]) for r in range(N)])
    uset = t if own is None else own["t"]
    h = np.zeros((N, 128, 4 * NC), BF)
    for c in range(N):
        for r in range(N):
            P = layer(w2[r], [mx_ref.quantize(uset[r][c])])
            Z = P if r == 0 else [z + p for z, p in zip(Z, P)]
        h[c] = tile(act2(Z))
    use = h if own is None else own["h"]
    H = [mx_ref.quantize(use[j]) for j in range(N)]
    y = np.zeros((N, 128, N * G * NC), np.float32)
    for r in range(N):
        for j in range(N):
            Z = layer(w3[r], [H[j]])
            for i in range(G):
                y[r][:, NC * (G * j + i):NC * (G * j + i) + NC] = Z[i]
    return {"t": t, "h": h, "y": y}

@@ -1,0 +1,322 @@
+from concourse.bass import DstId, RemoteDMATransfer
+from concourse.mybir import dt, AluOpType, ActivationFunctionType as AF
+
+NC = 128
+C1, C2 = 0.041, 0.0145
+
+SCRATCH = {
+    "xin": ("sbuf", [128, 512], "bfloat16"),
+    "w1in": ("sbuf", [128, 1024], "bfloat16"),
+    "w2in": ("sbuf", [128, 1024], "bfloat16"),
+    "w3in": ("sbuf", [128, 1024], "bfloat16"),
+    "xc": ("sbuf", [128, 1024], "float8_e4m3fn_x4"), "xs": ("sbuf", [128, 1024], "uint8"),
+    "hc": ("sbuf", [128, 1024], "float8_e4m3fn_x4"), "hs": ("sbuf", [128, 1024], "uint8"),
+    "w1c": ("sbuf", [128, 256], "float8_e4m3fn_x4"), "w1s": ("sbuf", [128, 256], "uint8"),
+    "w2c": ("sbuf", [128, 1024], "float8_e4m3fn_x4"), "w2s": ("sbuf", [128, 1024], "uint8"),
+    "w3c": ("sbuf", [128, 256], "float8_e4m3fn_x4"), "w3s": ("sbuf", [128, 256], "uint8"),
+    "tt": ("sbuf", [128, 4096], "bfloat16"),
+    "tc": ("sbuf", [128, 1024], "float8_e4m3fn_x4"), "ts": ("sbuf", [128, 1024], "uint8"),
+    "rc": ("sbuf", [128, 1024], "float8_e4m3fn_x4"), "rs": ("sbuf", [128, 1024], "uint8"),
+    "pf": ("sbuf", [128, 256], "float32"),
+    "pin": ("sbuf", [128, 256], "float32"),
+    "sf": ("sbuf", [128, 256], "float32"),
+    "hb": ("sbuf", [128, 512], "bfloat16"),
+    "yb": ("sbuf", [128, 2048], "float32"),
+    "ps": ("psum", [128, 4096], "float32"),
+}
+SEMAPHORES = (
+    ["lx", "lw1", "lw2", "lw3", "st"]
+    + ["qx", "qw1", "qw2", "qw3", "qth", "qtp", "qtn", "qh"]
+    + ["zh0", "zh1", "zp0", "zp1", "zn0", "zn1", "sumh", "sumf"]
+    + ["ash", "avh", "asp", "avp", "asn", "avn", "pf0", "pf1"]
+    + ["ad0", "ad1", "hs0", "hv0"]
+    + ["axh", "axp", "axn", "aw2", "at", "apin", "ahi", "ahq", "ahp", "ahn"]
+    + ["rxc", "rxs", "rp", "rhc", "rhs"]
+    + ["ly%d%d" % (p, i) for p in range(4) for i in range(2)]
+    + ["yc%d" % p for p in range(4)]
+    + ["loct", "locp", "loch"]
+)
+
+
+def bits(m):
+    return [b for b in range(16) if m >> b & 1]
+
+
+def setof(bs):
+    return sum(1 << b for b in bs)
+
+
+def plan(T, topo):
+    cores = list(T.cores)
+    P = {}
+    for ch in sorted(set(topo.chip(c) for c in cores)):
+        home = [c for c in cores if topo.chip(c) == ch]
+        away = [c for c in cores if topo.chip(c) != ch]
+        port = [c for c in home if topo.may_write(c, away[0])]
+        helpers = [c for c in range(128) if topo.chip(c) == ch and c not in cores]
+        relay = [c for c in helpers if topo.may_write(c, away[0])]
+        P[ch] = dict(home=home, away=away, port=port, inner=[c for c in home if c not in port],
+                     relay=relay, fan=[c for c in helpers if c not in relay])
+    return P
+
+
+def rank_program(g, core, T, topo):
+    S = T.sem
+    P = plan(T, topo)
+    ch = topo.chip(core)
+    if ch not in P:
+        return
+    me = P[ch]
+    other = P[[k for k in P if k != ch][0]]
+    home, away = me["home"], me["away"]
+    slot = {c: i for i, c in enumerate(T.cores)}
+    FULL = topo.mask(home[0], home[1])
+    LO = topo.mask(me["port"][0], away[0])
+    HI = FULL & ~LO
+    EVEN, ODD = setof(bits(FULL)[0::2]), setof(bits(FULL)[1::2])
+    U8 = dt.uint8
+
+    def did(c):
+        a = topo.addr(c)
+        return DstId(rid=a[0], pnc=a[1])
+
+    def send(moves, loc):
+        g.remote_dma_fused([RemoteDMATransfer(dst_ids=[did(c) for c in ds], dma_engine_mask=m, remote_sem=rs, srcs=[src],
+                                              dsts=[dst] * len(ds)) for m, ds, rs, src, dst in moves], local_sem=loc)
+        return sum(len(bits(m)) for m, ds, rs, src, dst in moves)
+
+    def cv(buf, a, b):
+        return buf[:, a:b].bitcast(U8)
+
+    def cols(cs):
+        a = NC * min(slot[c] for c in cs)
+        return a, a + NC * len(cs)
+
+    ia, ib = cols(me["inner"])
+
+    if core in me["relay"]:
+        k = me["relay"].index(core)
+        dst = away[2 * k:2 * k + 2]
+        n = 0
+        g.wait_ge(S.rxs, 16)
+        n += send([(LO, dst, S.axn, T.xs[:, ia:ib], T.xs[:, ia:ib])], S.loct)
+        g.wait_ge(S.rxc, 16)
+        n += send([(LO, dst, S.axn, cv(T.xc, ia, ib), cv(T.xc, ia, ib))], S.loct)
+        g.wait_ge(S.rp, 16)
+        n += send([(LO, [other["port"][k]], S.apin, T.pin[:], T.pin[:])], S.loct)
+        g.wait_ge(S.rhs, 16)
+        n += send([(LO, dst, S.ahn, T.hs[:, ia:ib], T.hs[:, ia:ib])], S.loct)
+        g.wait_ge(S.rhc, 16)
+        n += send([(LO, dst, S.ahn, cv(T.hc, ia, ib), cv(T.hc, ia, ib))], S.loct)
+        g.wait_ge(S.loct, n)
+        return
+    if core in me["fan"]:
+        a, b = cols([other["port"][me["fan"].index(core)]])
+        n = 0
+        for c_, s_, sc, ss, dd in ((T.xc, T.xs, S.rxc, S.rxs, S.axp), (T.hc, T.hs, S.rhc, S.rhs, S.ahp)):
+            g.wait_ge(ss, 8)
+            n += send([(FULL, home, dd, s_[:, a:b], s_[:, a:b])], S.loct)
+            g.wait_ge(sc, 8)
+            n += send([(FULL, home, dd, cv(c_, a, b), cv(c_, a, b))], S.loct)
+        g.wait_ge(S.loct, n)
+        return
+    if core not in home:
+        return
+
+    peers = [c for c in home if c != core]
+    lr = home.index(core)
+    isport = core in me["port"]
+    k = me["port" if isport else "inner"].index(core)
+    mate = other["inner" if isport else "port"][k]
+    owner = {}
+    for kind, by in (("inner", "port"), ("port", "inner")):
+        for c, o in zip(other[kind], me[by]):
+            owner[c] = o
+    tcol = {}
+    for c in home:
+        tcol[c] = 2 * NC * home.index(c)
+    for c in away:
+        tcol[c] = 2 * NC * home.index(owner[c]) + NC
+    a0, a1 = cols([core])
+    h0, h1 = cols(home)
+    p0, p1 = cols(other["port"])
+    n0, n1 = cols(other["inner"])
+    w0 = 2 * NC * lr
+    ps = T.ps
+
+    def bank(b, n, a=0):
+        return ps[:, 512 * b + a:512 * b + a + n]
+
+    sy = g.sync
+    sy.dma_start(T.xin[:], T.x[:]).then_inc(S.lx, 16)
+    sy.wait_ge(S.lx, 16)
+    sy.dma_start(T.w1in[:], T.w1[:]).then_inc(S.lw1, 16)
+    sy.dma_start(T.w2in[:], T.w2[:]).then_inc(S.lw2, 16)
+
+    def gather(c_, s_, sc, ss, hh, loc):
+        n = 0
+        for src, hs in ((s_[:, a0:a1], ss), (cv(c_, a0, a1), sc)):
+            if isport:
+                n += send([(LO, [other["fan"][k]], hs, src, src), (HI, peers, hh, src, src)], loc)
+            else:
+                n += send([(EVEN, me["relay"], hs, src, src), (ODD, peers, hh, src, src)], loc)
+        return n
+
+    def exchange(owners):
+        n = 0
+        ds = [o for o in owners if o != core]
+        masks = [FULL] if len(ds) == 1 else [EVEN, ODD]
+        for cod in (1, 0):
+            mv = []
+            for m, o in zip(masks, ds):
+                ta = 2 * NC * home.index(o)
+                if cod:
+                    mv.append((m, [o], S.at, cv(T.tc, ta, ta + 2 * NC), cv(T.rc, w0, w0 + 2 * NC)))
+                else:
+                    mv.append((m, [o], S.at, T.ts[:, ta:ta + 2 * NC], T.rs[:, w0:w0 + 2 * NC]))
+            n += send(mv, S.loct)
+        return n
+    g.wait_ge(S.qx, 1)
+    nl = gather(T.xc, T.xs, S.rxc, S.rxs, S.axh, S.loct)
+    g.wait_ge(S.qw2, 1)
+    for src in (cv(T.w2c, w0, w0 + 2 * NC), T.w2s[:, w0:w0 + 2 * NC]):
+        nl += send([(FULL, peers, S.aw2, src, src)], S.loct)
+    g.wait_ge(S.qth, 4)
+    g.wait_ge(S.qtp, 2)
+    nl += exchange(me["inner"])
+    g.wait_ge(S.qtn, 2)
+    nl += exchange(me["port"])
+    g.wait_ge(S.pf0, 1)
+    g.wait_ge(S.pf1, 1)
+    if isport:
+        nlp = send([(LO, [mate], S.apin, T.pf[:], T.pin[:])], S.locp)
+    else:
+        nlp = send([(FULL, [me["relay"][k]], S.rp, T.pf[:], T.pin[:])], S.locp)
+    g.wait_ge(S.qh, 1)
+    nlh = gather(T.hc, T.hs, S.rhc, S.rhs, S.ahq if isport else S.ahi, S.loch)
+    g.wait_ge(S.loch, nlh)
+
+    te = g.tensor
+
+    def mm(b, wc, ws, w, mc, ms, a, n, st=True, sp=True):
+        return te.matmul_mx(bank(b, n), wc[:, w:w + NC], ws[:, w:w + NC], mc[:, a:a + n], ms[:, a:a + n], st, sp)
+    te.wait_ge(S.qw1, 1)
+    te.wait_ge(S.qx, 1)
+    te.wait_ge(S.axh, 3 * 16)
+    for i in (0, 1):
+        mm(i, T.w1c, T.w1s, NC * i, T.xc, T.xs, h0, 512).then_inc(S["zh%d" % i], 1)
+    te.wait_ge(S.axp, 2 * 32)
+    for i in (0, 1):
+        mm(2 + i, T.w1c, T.w1s, NC * i, T.xc, T.xs, p0, 256).then_inc(S["zp%d" % i], 1)
+    te.wait_ge(S.axn, 16)
+    te.wait_ge(S.ash, 2)
+    te.wait_ge(S.avh, 2)
+    for i in (0, 1):
+        mm(i, T.w1c, T.w1s, NC * i, T.xc, T.xs, n0, 256).then_inc(S["zn%d" % i], 1)
+
+    def chipsum(b, off, sem):
+        for i in (0, 1):
+            for q, r in enumerate([lr] + [home.index(p) for p in peers]):
+                mc, ms = (T.tc, T.ts) if r == lr else (T.rc, T.rs)
+                a = w0 + off if r == lr else 2 * NC * r + off
+                ins = mm(b + i, T.w2c, T.w2s, 2 * NC * r + NC * i, mc, ms, a, NC, q == 0, q == 3)
+                if q == 3:
+                    ins.then_inc(sem, 1)
+    te.wait_ge(S.qw2, 1)
+    te.wait_ge(S.aw2, 3 * 32)
+    te.wait_ge(S.qth, 4)
+    te.wait_ge(S.qtn if isport else S.qtp, 2)
+    te.wait_ge(S.at, 64)
+    chipsum(6, NC, S.sumf)
+    chipsum(4, 0, S.sumh)
+    ypairs = ((me["inner"], 0), (me["port"], 2), (other["port"], 6), (other["inner"], 4))
+    before = (
+        ((S.ahi, 16 * len([c for c in me["inner"] if c != core])), (S.asn, 2), (S.avn, 2)),
+        ((S.ahq, 16 * len([c for c in me["port"] if c != core])), (S.asp, 2), (S.avp, 2)),
+        ((S.ahp, 2 * 32), (S.pf0, 1), (S.pf1, 1)),
+        ((S.ahn, 16), (S.ad0, 1), (S.ad1, 1)))
+    te.wait_ge(S.qw3, 1)
+    te.wait_ge(S.qh, 1)
+    for p, (grp, b) in enumerate(ypairs):
+        for sem, v in before[p]:
+            te.wait_ge(sem, v)
+        g0 = cols(grp)[0]
+        for i in (0, 1):
+            mm(b + i, T.w3c, T.w3s, NC * i, T.hc, T.hs, g0, 256).then_inc(S["ly%d%d" % (p, i)], 1)
+
+    sc, ve = g.scalar, g.vector
+
+    def act_s(src, n, out, c0, c, sem):
+        for q, sg in ((0, 1.0), (1, -1.0)):
+            sc.activation(out[:, 4 * c0 + q:4 * c0 + 4 * n:4], src, AF.Relu, scale=sg * c).then_inc(sem, 1)
+
+    def act_v(src, n, out, c0, c, sem):
+        for q, sg in ((2, 1.0), (3, -1.0)):
+            ve.tensor_scalar(out[:, 4 * c0 + q:4 * c0 + 4 * n:4], src, sg * c, 0.0, AluOpType.mult, AluOpType.max).then_inc(sem, 1)
+    ve.wait_ge(S.lx, 16)
+    ve.quantize_mx(T.xc[:, a0:a1], T.xs[:, a0:a1], T.xin[:]).then_inc(S.qx, 1)
+    ve.wait_ge(S.lw1, 16)
+    ve.quantize_mx(T.w1c[:], T.w1s[:], T.w1in[:]).then_inc(S.qw1, 1)
+    ve.wait_ge(S.lw2, 16)
+    ve.quantize_mx(T.w2c[:, w0:w0 + 2 * NC], T.w2s[:, w0:w0 + 2 * NC], T.w2in[:]).then_inc(S.qw2, 1)
+    for tag, b, n, c0, grp in (("h", 0, 512, h0, home), ("p", 2, 256, p0, other["port"]), ("n", 0, 256, n0, other["inner"])):
+        sc.wait_ge(S["z%s0" % tag], 1)
+        act_s(bank(b, n), n, T.tt, c0, C1, S["as" + tag])
+        ve.wait_ge(S["z%s1" % tag], 1)
+        act_v(bank(b + 1, n), n, T.tt, c0, C1, S["av" + tag])
+        ve.wait_ge(S["av" + tag], 2)
+        ve.wait_ge(S["as" + tag], 2)
+        for c in grp:
+            u, v = 4 * NC * slot[c], tcol[c]
+            ve.quantize_mx(T.tc[:, v:v + NC], T.ts[:, v:v + NC], T.tt[:, u:u + 4 * NC]).then_inc(S["qt" + tag], 1)
+    sc.wait_ge(S.sumf, 2)
+    sc.activation(T.pf[:, 0:NC], bank(6, NC), AF.Copy).then_inc(S.pf0, 1)
+    ve.wait_ge(S.sumf, 2)
+    ve.tensor_copy(T.pf[:, NC:2 * NC], bank(7, NC)).then_inc(S.pf1, 1)
+    ve.wait_ge(S.lw3, 16)
+    ve.quantize_mx(T.w3c[:], T.w3s[:], T.w3in[:]).then_inc(S.qw3, 1)
+    ve.wait_ge(S.sumh, 2)
+    ve.wait_ge(S.apin, 8)
+    for i in (0, 1):
+        ve.tensor_tensor(T.sf[:, NC * i:NC * i + NC], bank(4 + i, NC), T.pin[:, NC * i:NC * i + NC],
+                         AluOpType.add).then_inc(S["ad%d" % i], 1)
+    sc.wait_ge(S.ad0, 1)
+    act_s(T.sf[:, 0:NC], NC, T.hb, 0, C2, S.hs0)
+    ve.wait_ge(S.ad1, 1)
+    act_v(T.sf[:, NC:2 * NC], NC, T.hb, 0, C2, S.hv0)
+    ve.wait_ge(S.hs0, 2)
+    ve.wait_ge(S.hv0, 2)
+    ve.quantize_mx(T.hc[:, a0:a1], T.hs[:, a0:a1], T.hb[:]).then_inc(S.qh, 1)
+    for p, (grp, b) in enumerate(ypairs):
+        sc.wait_ge(S["ly%d0" % p], 1)
+        ve.wait_ge(S["ly%d1" % p], 1)
+        g0 = cols(grp)[0]
+        for q in (0, 1):
+            o = 2 * (g0 + NC * q)
+            sc.activation(T.yb[:, o:o + NC], bank(b, NC, NC * q), AF.Copy).then_inc(S["yc%d" % p], 1)
+            ve.tensor_copy(T.yb[:, o + NC:o + 2 * NC], bank(b + 1, NC, NC * q)).then_inc(S["yc%d" % p], 1)
+
+    nst = [0]
+
+    def store(out, in_):
+        sy.dma_start(out, in_).then_inc(S.st, 16)
+        nst[0] += 16
+
+    def tstore(cs):
+        for c in cs:
+            store(T.t[slot[c]], T.tt[:, 4 * NC * slot[c]:4 * NC * slot[c] + 4 * NC])
+    sy.wait_ge(S.qth, 4)
+    tstore(home)
+    sy.wait_ge(S.loct, nl)
+    sy.dma_start(T.w3in[:], T.w3[:]).then_inc(S.lw3, 16)
+    sy.wait_ge(S.locp, nlp)
+    sy.wait_ge(S.qtp, 2)
+    sy.wait_ge(S.qtn, 2)
+    tstore(away)
+    sy.wait_ge(S.loch, nlh)
+    store(T.h[:], T.hb[:])
+    for p, (grp, b) in enumerate(ypairs):
+        sy.wait_ge(S["yc%d" % p], 4)
+        g0, g1 = cols(grp)
+        store(T.y[:, 2 * g0:2 * g1], T.yb[:, 2 * g0:2 * g1])
+    sy.wait_ge(S.st, nst[0])

@@ -4,38 +4,36 @@ from concourse.mybir import dt, AluOpType, ActivationFunctionType as AF
 NC = 128
 C1, C2 = 0.041, 0.0145
 
+BFT, CODES, F32 = "bfloat16", "float8_e4m3fn_x4", "float32"
 SCRATCH = {
-    "xin": ("sbuf", [128, 512], "bfloat16"),
-    "w1in": ("sbuf", [128, 1024], "bfloat16"),
-    "w2in": ("sbuf", [128, 1024], "bfloat16"),
-    "w3in": ("sbuf", [128, 1024], "bfloat16"),
-    "xc": ("sbuf", [128, 1024], "float8_e4m3fn_x4"), "xs": ("sbuf", [128, 1024], "uint8"),
-    "hc": ("sbuf", [128, 1024], "float8_e4m3fn_x4"), "hs": ("sbuf", [128, 1024], "uint8"),
-    "w1c": ("sbuf", [128, 256], "float8_e4m3fn_x4"), "w1s": ("sbuf", [128, 256], "uint8"),
-    "w2c": ("sbuf", [128, 1024], "float8_e4m3fn_x4"), "w2s": ("sbuf", [128, 1024], "uint8"),
-    "w3c": ("sbuf", [128, 256], "float8_e4m3fn_x4"), "w3s": ("sbuf", [128, 256], "uint8"),
-    "tt": ("sbuf", [128, 4096], "bfloat16"),
-    "tc": ("sbuf", [128, 1024], "float8_e4m3fn_x4"), "ts": ("sbuf", [128, 1024], "uint8"),
-    "rc": ("sbuf", [128, 1024], "float8_e4m3fn_x4"), "rs": ("sbuf", [128, 1024], "uint8"),
-    "pf": ("sbuf", [128, 256], "float32"),
-    "pin": ("sbuf", [128, 256], "float32"),
-    "sf": ("sbuf", [128, 256], "float32"),
-    "hb": ("sbuf", [128, 512], "bfloat16"),
-    "yb": ("sbuf", [128, 2048], "float32"),
-    "ps": ("psum", [128, 4096], "float32"),
+    "xin": ("sbuf", [128, 512], BFT),
+    "tt": ("sbuf", [128, 4096], BFT),
+    "hb": ("sbuf", [128, 512], BFT),
+    "pf": ("sbuf", [128, 256], F32),
+    "pin": ("sbuf", [128, 256], F32),
+    "sf": ("sbuf", [128, 256], F32),
+    "yb": ("sbuf", [128, 2048], F32),
+    "ps": ("psum", [128, 4096], F32),
 }
+for _w in ("w1in", "w2in", "w3in"):
+    SCRATCH[_w] = ("sbuf", [128, 1024], BFT)
+for _n, _c in (("x", 1024), ("h", 1024), ("w1", 256), ("w2", 1024), ("w3", 256), ("t", 1024), ("r", 1024)):
+    SCRATCH[_n + "c"] = ("sbuf", [128, _c], CODES)
+    SCRATCH[_n + "s"] = ("sbuf", [128, _c], "uint8")
+GROUPS = "oiqpn"
 SEMAPHORES = (
     ["lx", "lw1", "lw2", "lw3", "st"]
-    + ["qx", "qw1", "qw2", "qw3", "qth", "qtp", "qtn", "qh"]
-    + ["zh0", "zh1", "zp0", "zp1", "zn0", "zn1", "sumh", "sumf"]
-    + ["ash", "avh", "asp", "avp", "asn", "avn", "pf0", "pf1"]
+    + ["qx", "qw1", "qw2", "qw3", "qh"] + ["qt" + a for a in GROUPS]
+    + ["z%s%d" % (a, i) for a in GROUPS for i in range(2)]
+    + ["a%s%s" % (e, a) for a in GROUPS for e in "sv"]
+    + ["sumh0", "sumh1", "sumf0", "sumf1", "pf0", "pf1"]
     + ["ad0", "ad1", "hs0", "hv0"]
-    + ["axh", "axp", "axn", "aw2", "at", "apin", "ahi", "ahq", "ahp", "ahn"]
-    + ["rxc", "rxs", "rp", "rhc", "rhs"]
+    + ["axi", "axq", "axp", "axn", "aw2", "apin0", "apin1", "ahi", "ahq", "ahp", "ahn"]
+    + ["at%d" % r for r in range(4)]
+    + ["rxc", "rxs", "rp0", "rp1", "rhc", "rhs", "uxc", "uxs", "uhc", "uhs"]
     + ["ly%d%d" % (p, i) for p in range(4) for i in range(2)]
     + ["yc%d" % p for p in range(4)]
-    + ["loct", "locp", "loch"]
-)
+    + ["loct", "locp", "loch"])
 
 
 def bits(m):
@@ -72,9 +70,8 @@ def rank_program(g, core, T, topo):
     slot = {c: i for i, c in enumerate(T.cores)}
     FULL = topo.mask(home[0], home[1])
     LO = topo.mask(me["port"][0], away[0])
-    HI = FULL & ~LO
     EVEN, ODD = setof(bits(FULL)[0::2]), setof(bits(FULL)[1::2])
-    U8 = dt.uint8
+    nfull, nlo, nev = len(bits(FULL)), len(bits(LO)), len(bits(EVEN))
 
     def did(c):
         a = topo.addr(c)
@@ -86,44 +83,47 @@ def rank_program(g, core, T, topo):
         return sum(len(bits(m)) for m, ds, rs, src, dst in moves)
 
     def cv(buf, a, b):
-        return buf[:, a:b].bitcast(U8)
+        return buf[:, a:b].bitcast(dt.uint8)
 
     def cols(cs):
         a = NC * min(slot[c] for c in cs)
         return a, a + NC * len(cs)
 
-    ia, ib = cols(me["inner"])
+    def passon(t, pre, rank, need, mask, ds, ss, sc):
+        a, b = cols([rank])
+        g.wait_ge(S[pre + t + "s"], need)
+        v = T[t + "s"][:, a:b]
+        n = send([(mask, ds, S[ss], v, v)], S.loct)
+        g.wait_ge(S[pre + t + "c"], need)
+        v = cv(T[t + "c"], a, b)
+        return n + send([(mask, ds, S[sc], v, v)], S.loct)
 
+    tosend = {"x": EVEN, "h": FULL}
     if core in me["relay"]:
         k = me["relay"].index(core)
-        dst = away[2 * k:2 * k + 2]
         n = 0
-        g.wait_ge(S.rxs, 16)
-        n += send([(LO, dst, S.axn, T.xs[:, ia:ib], T.xs[:, ia:ib])], S.loct)
-        g.wait_ge(S.rxc, 16)
-        n += send([(LO, dst, S.axn, cv(T.xc, ia, ib), cv(T.xc, ia, ib))], S.loct)
-        g.wait_ge(S.rp, 16)
-        n += send([(LO, [other["port"][k]], S.apin, T.pin[:], T.pin[:])], S.loct)
-        g.wait_ge(S.rhs, 16)
-        n += send([(LO, dst, S.ahn, T.hs[:, ia:ib], T.hs[:, ia:ib])], S.loct)
-        g.wait_ge(S.rhc, 16)
-        n += send([(LO, dst, S.ahn, cv(T.hc, ia, ib), cv(T.hc, ia, ib))], S.loct)
+        for t in "xh":
+            n += passon(t, "r", me["inner"][k], len(bits(tosend[t])), LO, [other["relay"][k]], "u%ss" % t, "u%sc" % t)
+            n += passon(t, "u", other["inner"][k], nlo, FULL, home, "a%sn" % t, "a%sn" % t)
+            if t == "x":
+                for i in (0, 1):
+                    v = T.pin[:, NC * i:NC * i + NC]
+                    g.wait_ge(S["rp%d" % i], nfull)
+                    n += send([(LO, [other["port"][k]], S["apin%d" % i], v, v)], S.loct)
         g.wait_ge(S.loct, n)
         return
     if core in me["fan"]:
-        a, b = cols([other["port"][me["fan"].index(core)]])
+        k = me["fan"].index(core)
         n = 0
-        for c_, s_, sc, ss, dd in ((T.xc, T.xs, S.rxc, S.rxs, S.axp), (T.hc, T.hs, S.rhc, S.rhs, S.ahp)):
-            g.wait_ge(ss, 8)
-            n += send([(FULL, home, dd, s_[:, a:b], s_[:, a:b])], S.loct)
-            g.wait_ge(sc, 8)
-            n += send([(FULL, home, dd, cv(c_, a, b), cv(c_, a, b))], S.loct)
+        for t in "xh":
+            n += passon(t, "r", other["port"][k], nlo, FULL, home, "a%sp" % t, "a%sp" % t)
         g.wait_ge(S.loct, n)
         return
     if core not in home:
         return
 
     peers = [c for c in home if c != core]
+    ipeers, qpeers = [c for c in me["inner"] if c != core], [c for c in me["port"] if c != core]
     lr = home.index(core)
     isport = core in me["port"]
     k = me["port" if isport else "inner"].index(core)
@@ -138,9 +138,6 @@ def rank_program(g, core, T, topo):
     for c in away:
         tcol[c] = 2 * NC * home.index(owner[c]) + NC
     a0, a1 = cols([core])
-    h0, h1 = cols(home)
-    p0, p1 = cols(other["port"])
-    n0, n1 = cols(other["inner"])
     w0 = 2 * NC * lr
     ps = T.ps
 
@@ -149,92 +146,97 @@ def rank_program(g, core, T, topo):
 
     sy = g.sync
     sy.dma_start(T.xin[:], T.x[:]).then_inc(S.lx, 16)
-    sy.wait_ge(S.lx, 16)
     sy.dma_start(T.w1in[:], T.w1[:]).then_inc(S.lw1, 16)
+    sy.wait_ge(S.lx, 16)
     sy.dma_start(T.w2in[:], T.w2[:]).then_inc(S.lw2, 16)
 
-    def gather(c_, s_, sc, ss, hh, loc):
+    def gather(t, hh, loc):
+        mask, helper = (LO, other["fan"][k]) if isport else (tosend[t], me["relay"][k])
+        pieces = ((T[t + "s"][:, a0:a1], S["r%ss" % t]), (cv(T[t + "c"], a0, a1), S["r%sc" % t]))
         n = 0
-        for src, hs in ((s_[:, a0:a1], ss), (cv(c_, a0, a1), sc)):
-            if isport:
-                n += send([(LO, [other["fan"][k]], hs, src, src), (HI, peers, hh, src, src)], loc)
-            else:
-                n += send([(EVEN, me["relay"], hs, src, src), (ODD, peers, hh, src, src)], loc)
+        for src, hs in pieces:
+            n += send([(mask, [helper], hs, src, src)], loc)
+        for src, hs in pieces:
+            n += send([(FULL, peers, hh, src, src)], loc)
         return n
 
     def exchange(owners):
         n = 0
         ds = [o for o in owners if o != core]
         masks = [FULL] if len(ds) == 1 else [EVEN, ODD]
+        sem = S["at%d" % lr]
         for cod in (1, 0):
             mv = []
             for m, o in zip(masks, ds):
                 ta = 2 * NC * home.index(o)
                 if cod:
-                    mv.append((m, [o], S.at, cv(T.tc, ta, ta + 2 * NC), cv(T.rc, w0, w0 + 2 * NC)))
+                    mv.append((m, [o], sem, cv(T.tc, ta, ta + 2 * NC), cv(T.rc, w0, w0 + 2 * NC)))
                 else:
-                    mv.append((m, [o], S.at, T.ts[:, ta:ta + 2 * NC], T.rs[:, w0:w0 + 2 * NC]))
+                    mv.append((m, [o], sem, T.ts[:, ta:ta + 2 * NC], T.rs[:, w0:w0 + 2 * NC]))
             n += send(mv, S.loct)
         return n
+    qt_home = ((S.qto, 1), (S.qti, len(ipeers)), (S.qtq, len(qpeers)))
     g.wait_ge(S.qx, 1)
-    nl = gather(T.xc, T.xs, S.rxc, S.rxs, S.axh, S.loct)
+    nl = gather("x", S.axq if isport else S.axi, S.loct)
     g.wait_ge(S.qw2, 1)
     for src in (cv(T.w2c, w0, w0 + 2 * NC), T.w2s[:, w0:w0 + 2 * NC]):
         nl += send([(FULL, peers, S.aw2, src, src)], S.loct)
-    g.wait_ge(S.qth, 4)
+    for sem, v in qt_home:
+        g.wait_ge(sem, v)
     g.wait_ge(S.qtp, 2)
     nl += exchange(me["inner"])
     g.wait_ge(S.qtn, 2)
     nl += exchange(me["port"])
-    g.wait_ge(S.pf0, 1)
-    g.wait_ge(S.pf1, 1)
-    if isport:
-        nlp = send([(LO, [mate], S.apin, T.pf[:], T.pin[:])], S.locp)
-    else:
-        nlp = send([(FULL, [me["relay"][k]], S.rp, T.pf[:], T.pin[:])], S.locp)
+    nlp = 0
+    for i in (0, 1):
+        v, w = T.pf[:, NC * i:NC * i + NC], T.pin[:, NC * i:NC * i + NC]
+        g.wait_ge(S["pf%d" % i], 1)
+        if isport:
+            nlp += send([(LO, [mate], S["apin%d" % i], v, w)], S.locp)
+        else:
+            nlp += send([(FULL, [me["relay"][k]], S["rp%d" % i], v, w)], S.locp)
     g.wait_ge(S.qh, 1)
-    nlh = gather(T.hc, T.hs, S.rhc, S.rhs, S.ahq if isport else S.ahi, S.loch)
+    nlh = gather("h", S.ahq if isport else S.ahi, S.loch)
     g.wait_ge(S.loch, nlh)
 
     te = g.tensor
 
     def mm(b, wc, ws, w, mc, ms, a, n, st=True, sp=True):
         return te.matmul_mx(bank(b, n), wc[:, w:w + NC], ws[:, w:w + NC], mc[:, a:a + n], ms[:, a:a + n], st, sp)
+    both = 2 * nfull
+    groups = (("o", [core], 0, ()),
+              ("i", ipeers, 2, ((S.axi, both * len(ipeers)),)),
+              ("q", qpeers, 4, ((S.axq, both * len(qpeers)),)),
+              ("p", other["port"], 6, ((S.axp, both * 2),)),
+              ("n", other["inner"], 0, ((S.axn, both * 2), (S.aso, 2), (S.avo, 2))))
     te.wait_ge(S.qw1, 1)
     te.wait_ge(S.qx, 1)
-    te.wait_ge(S.axh, 3 * 16)
-    for i in (0, 1):
-        mm(i, T.w1c, T.w1s, NC * i, T.xc, T.xs, h0, 512).then_inc(S["zh%d" % i], 1)
-    te.wait_ge(S.axp, 2 * 32)
-    for i in (0, 1):
-        mm(2 + i, T.w1c, T.w1s, NC * i, T.xc, T.xs, p0, 256).then_inc(S["zp%d" % i], 1)
-    te.wait_ge(S.axn, 16)
-    te.wait_ge(S.ash, 2)
-    te.wait_ge(S.avh, 2)
-    for i in (0, 1):
-        mm(i, T.w1c, T.w1s, NC * i, T.xc, T.xs, n0, 256).then_inc(S["zn%d" % i], 1)
-
-    def chipsum(b, off, sem):
+    for tag, grp, b, waits in groups:
+        for sem, v in waits:
+            te.wait_ge(sem, v)
+        ga, gb = cols(grp)
         for i in (0, 1):
-            for q, r in enumerate([lr] + [home.index(p) for p in peers]):
-                mc, ms = (T.tc, T.ts) if r == lr else (T.rc, T.rs)
-                a = w0 + off if r == lr else 2 * NC * r + off
-                ins = mm(b + i, T.w2c, T.w2s, 2 * NC * r + NC * i, mc, ms, a, NC, q == 0, q == 3)
-                if q == 3:
-                    ins.then_inc(sem, 1)
+            mm(b + i, T.w1c, T.w1s, NC * i, T.xc, T.xs, ga, gb - ga).then_inc(S["z%s%d" % (tag, i)], 1)
     te.wait_ge(S.qw2, 1)
-    te.wait_ge(S.aw2, 3 * 32)
-    te.wait_ge(S.qth, 4)
-    te.wait_ge(S.qtn if isport else S.qtp, 2)
-    te.wait_ge(S.at, 64)
-    chipsum(6, NC, S.sumf)
-    chipsum(4, 0, S.sumh)
+    te.wait_ge(S.aw2, 3 * both)
+    for sem, v in qt_home + ((S.qtp, 2), (S.qtn, 2)):
+        te.wait_ge(sem, v)
+    for q, c in enumerate([core] + ipeers + qpeers):
+        r = home.index(c)
+        if q:
+            te.wait_ge(S["at%d" % r], both if (c in me["port"]) == isport else 2 * nev)
+        mc, ms = (T.rc, T.rs) if q else (T.tc, T.ts)
+        for b, off, tag in ((6, NC, "f"), (4, 0, "h")):
+            for i in (0, 1):
+                ins = mm(b + i, T.w2c, T.w2s, 2 * NC * r + NC * i, mc, ms, 2 * NC * r + off, NC, q == 0, q == 3)
+                if q == 3:
+                    ins.then_inc(S["sum%s%d" % (tag, i)], 1)
     ypairs = ((me["inner"], 0), (me["port"], 2), (other["port"], 6), (other["inner"], 4))
     before = (
-        ((S.ahi, 16 * len([c for c in me["inner"] if c != core])), (S.asn, 2), (S.avn, 2)),
-        ((S.ahq, 16 * len([c for c in me["port"] if c != core])), (S.asp, 2), (S.avp, 2)),
-        ((S.ahp, 2 * 32), (S.pf0, 1), (S.pf1, 1)),
-        ((S.ahn, 16), (S.ad0, 1), (S.ad1, 1)))
+        ((S.ahi, both * len(ipeers)), (S.asn, 2), (S.avn, 2)),
+        ((S.ahq, both * len(qpeers)), (S.asi, 2), (S.avi, 2)),
+        ((S.ahp, both * 2), (S.pf0, 1), (S.pf1, 1)),
+        ((S.ahn, both * 2), (S.ad0, 1), (S.ad1, 1)))
     te.wait_ge(S.qw3, 1)
     te.wait_ge(S.qh, 1)
     for p, (grp, b) in enumerate(ypairs):
@@ -257,9 +259,8 @@ def rank_program(g, core, T, topo):
     ve.quantize_mx(T.xc[:, a0:a1], T.xs[:, a0:a1], T.xin[:]).then_inc(S.qx, 1)
     ve.wait_ge(S.lw1, 16)
     ve.quantize_mx(T.w1c[:], T.w1s[:], T.w1in[:]).then_inc(S.qw1, 1)
-    ve.wait_ge(S.lw2, 16)
-    ve.quantize_mx(T.w2c[:, w0:w0 + 2 * NC], T.w2s[:, w0:w0 + 2 * NC], T.w2in[:]).then_inc(S.qw2, 1)
-    for tag, b, n, c0, grp in (("h", 0, 512, h0, home), ("p", 2, 256, p0, other["port"]), ("n", 0, 256, n0, other["inner"])):
+    for tag, grp, b, waits in groups:
+        c0, n = cols(grp)[0], NC * len(grp)
         sc.wait_ge(S["z%s0" % tag], 1)
         act_s(bank(b, n), n, T.tt, c0, C1, S["as" + tag])
         ve.wait_ge(S["z%s1" % tag], 1)
@@ -269,15 +270,18 @@ def rank_program(g, core, T, topo):
         for c in grp:
             u, v = 4 * NC * slot[c], tcol[c]
             ve.quantize_mx(T.tc[:, v:v + NC], T.ts[:, v:v + NC], T.tt[:, u:u + 4 * NC]).then_inc(S["qt" + tag], 1)
-    sc.wait_ge(S.sumf, 2)
+        if tag == "o":
+            ve.wait_ge(S.lw2, 16)
+            ve.quantize_mx(T.w2c[:, w0:w0 + 2 * NC], T.w2s[:, w0:w0 + 2 * NC], T.w2in[:]).then_inc(S.qw2, 1)
+    sc.wait_ge(S.sumf0, 1)
     sc.activation(T.pf[:, 0:NC], bank(6, NC), AF.Copy).then_inc(S.pf0, 1)
-    ve.wait_ge(S.sumf, 2)
+    ve.wait_ge(S.sumf1, 1)
     ve.tensor_copy(T.pf[:, NC:2 * NC], bank(7, NC)).then_inc(S.pf1, 1)
     ve.wait_ge(S.lw3, 16)
     ve.quantize_mx(T.w3c[:], T.w3s[:], T.w3in[:]).then_inc(S.qw3, 1)
-    ve.wait_ge(S.sumh, 2)
-    ve.wait_ge(S.apin, 8)
     for i in (0, 1):
+        ve.wait_ge(S["sumh%d" % i], 1)
+        ve.wait_ge(S["apin%d" % i], nlo)
         ve.tensor_tensor(T.sf[:, NC * i:NC * i + NC], bank(4 + i, NC), T.pin[:, NC * i:NC * i + NC],
                          AluOpType.add).then_inc(S["ad%d" % i], 1)
     sc.wait_ge(S.ad0, 1)
@@ -305,7 +309,8 @@ def rank_program(g, core, T, topo):
     def tstore(cs):
         for c in cs:
             store(T.t[slot[c]], T.tt[:, 4 * NC * slot[c]:4 * NC * slot[c] + 4 * NC])
-    sy.wait_ge(S.qth, 4)
+    for sem, v in qt_home:
+        sy.wait_ge(sem, v)
     tstore(home)
     sy.wait_ge(S.loct, nl)
     sy.dma_start(T.w3in[:], T.w3[:]).then_inc(S.lw3, 16)

@@ -8,10 +8,11 @@ BFT, CODES, F32 = "bfloat16", "float8_e4m3fn_x4", "float32"
 SCRATCH = {
     "xin": ("sbuf", [128, 512], BFT),
     "tt": ("sbuf", [128, 4096], BFT),
-    "hb": ("sbuf", [128, 512], BFT),
-    "pf": ("sbuf", [128, 256], F32),
-    "pin": ("sbuf", [128, 256], F32),
-    "sf": ("sbuf", [128, 256], F32),
+    "hb": ("sbuf", [128, 1024], BFT),
+    "pf": ("sbuf", [128, 512], F32),
+    "pin": ("sbuf", [128, 512], F32),
+    "sf": ("sbuf", [128, 512], F32),
+    "sp": ("sbuf", [128, 256], F32),
     "yb": ("sbuf", [128, 2048], F32),
     "ps": ("psum", [128, 4096], F32),
 }
@@ -23,17 +24,19 @@ for _n, _c in (("x", 1024), ("h", 1024), ("w1", 256), ("w2", 1024), ("w3", 256),
 GROUPS = "oiqpn"
 SEMAPHORES = (
     ["lx", "lw1", "lw2", "lw3", "st"]
-    + ["qx", "qw1", "qw2", "qw3", "qh"] + ["qt" + a for a in GROUPS]
+    + ["qx", "qw1", "qw2", "qw3", "qh0", "qh1"] + ["qt" + a for a in GROUPS]
     + ["z%s%d" % (a, i) for a in GROUPS for i in range(2)]
     + ["a%s%s" % (e, a) for a in GROUPS for e in "sv"]
-    + ["sumh0", "sumh1", "sumf0", "sumf1", "pf0", "pf1"]
-    + ["ad0", "ad1", "hs0", "hv0"]
-    + ["axi", "axq", "axp", "axn", "aw2", "apin0", "apin1", "ahi", "ahq", "ahp", "ahn"]
+    + ["sum0", "sum1", "pf0", "pf1"]
+    + ["ad%d%d" % (j, i) for j in range(2) for i in range(2)]
+    + ["hs0", "hv0", "hs1", "hv1"]
+    + ["axi", "axq", "axp", "axn", "aw2", "full", "ahi", "ahq", "ahp", "ahn"]
     + ["at%d" % r for r in range(4)]
-    + ["rxc", "rxs", "rp0", "rp1", "rhc", "rhs", "uxc", "uxs", "uhc", "uhs"]
+    + ["rxc", "rxs", "uxc", "uxs"]
+    + ["rp0", "rp1", "me0", "me1", "ml0", "ml1"]
     + ["ly%d%d" % (p, i) for p in range(4) for i in range(2)]
     + ["yc%d" % p for p in range(4)]
-    + ["loct", "locp", "loch"])
+    + ["loct", "locp0", "locp1"])
 
 
 def bits(m):
@@ -70,8 +73,9 @@ def rank_program(g, core, T, topo):
     slot = {c: i for i, c in enumerate(T.cores)}
     FULL = topo.mask(home[0], home[1])
     LO = topo.mask(me["port"][0], away[0])
+    HI = FULL & ~LO
     EVEN, ODD = setof(bits(FULL)[0::2]), setof(bits(FULL)[1::2])
-    nfull, nlo, nev = len(bits(FULL)), len(bits(LO)), len(bits(EVEN))
+    nfull, nlo, nhi, nev = len(bits(FULL)), len(bits(LO)), len(bits(HI)), len(bits(EVEN))
 
     def did(c):
         a = topo.addr(c)
@@ -89,34 +93,82 @@ def rank_program(g, core, T, topo):
         a = NC * min(slot[c] for c in cs)
         return a, a + NC * len(cs)
 
-    def passon(t, pre, rank, need, mask, ds, ss, sc):
+    def plane(t, rank):
         a, b = cols([rank])
-        g.wait_ge(S[pre + t + "s"], need)
-        v = T[t + "s"][:, a:b]
-        n = send([(mask, ds, S[ss], v, v)], S.loct)
-        g.wait_ge(S[pre + t + "c"], need)
-        v = cv(T[t + "c"], a, b)
-        return n + send([(mask, ds, S[sc], v, v)], S.loct)
+        return T[t + "s"][:, a:b]
 
-    tosend = {"x": EVEN, "h": FULL}
+    def codes(t, rank):
+        a, b = cols([rank])
+        return cv(T[t + "c"], a, b)
+
+    def pass1(sem, need, v, mask, ds, to):
+        g.wait_ge(S[sem], need)
+        return send([(mask, ds, S[to], v, v)], S.loct)
+
+    sc, ve = g.scalar, g.vector
+
+    def act(eng, src, n, out, c0, c, q, sem):
+        o = out[:, 4 * c0 + q:4 * c0 + 4 * n:4]
+        sg = -c if q % 2 else c
+        if eng is sc:
+            sc.activation(o, src, AF.Relu, scale=sg).then_inc(sem, 1)
+        else:
+            ve.tensor_scalar(o, src, sg, 0.0, AluOpType.mult, AluOpType.max).then_inc(sem, 1)
+
+    def make_h(terms, full, rank, j, done):
+        ns = 2
+        if terms:
+            ns = 3
+            for i in (0, 1):
+                ve.tensor_tensor(full[:, NC * i:NC * i + NC], terms[i][0], terms[i][1], AluOpType.add).then_inc(S["ad%d%d" % (j, i)], 1)
+            sc.wait_ge(S["ad%d0" % j], 1)
+            ve.wait_ge(S["ad%d1" % j], 1)
+        for q in range(4):
+            if q == 2 and terms:
+                sc.wait_ge(S["ad%d1" % j], 1)
+            act(sc if q < ns else ve, full[:, NC * (q // 2):NC * (q // 2) + NC], NC, T.hb, NC * j, C2, q,
+                S["hs%d" % j] if q < ns else S["hv%d" % j])
+        ve.wait_ge(S["hs%d" % j], ns)
+        ve.wait_ge(S["hv%d" % j], 4 - ns)
+        a, b = cols([rank])
+        ve.quantize_mx(T.hc[:, a:b], T.hs[:, a:b], T.hb[:, 4 * NC * j:4 * NC * j + 4 * NC]).then_inc(done, 1)
+
+    def maker(j, rank, early, need, late, to):
+        o = 2 * NC * j
+        ve.wait_ge(S[early], need)
+        ve.wait_ge(S["ml%d" % j], late)
+        sums = T.sf[:, o:o + 2 * NC]
+        make_h([(T.pf[:, o + NC * i:o + NC * i + NC], T.pin[:, o + NC * i:o + NC * i + NC]) for i in (0, 1)], sums, rank, j, S["qh%d" % j])
+        n = 0
+        if rank in home:
+            for i in (0, 1):
+                g.wait_ge(S["ad%d%d" % (j, i)], 1)
+            n += send([(FULL, [rank], S.full, sums, T.sp[:])], S.loct)
+        g.wait_ge(S["qh%d" % j], 1)
+        for v in (plane("h", rank), codes("h", rank)):
+            n += send([(FULL, [c for c in home if c != rank], S[to], v, v)], S.loct)
+        return n
+
     if core in me["relay"]:
         k = me["relay"].index(core)
-        n = 0
-        for t in "xh":
-            n += passon(t, "r", me["inner"][k], len(bits(tosend[t])), LO, [other["relay"][k]], "u%ss" % t, "u%sc" % t)
-            n += passon(t, "u", other["inner"][k], nlo, FULL, home, "a%sn" % t, "a%sn" % t)
-            if t == "x":
-                for i in (0, 1):
-                    v = T.pin[:, NC * i:NC * i + NC]
-                    g.wait_ge(S["rp%d" % i], nfull)
-                    n += send([(LO, [other["port"][k]], S["apin%d" % i], v, v)], S.loct)
+        mine, theirs = me["inner"][k], other["inner"][k]
+        n = pass1("rxs", nev, plane("x", mine), LO, [other["fan"][k]], "uxs")
+        n += pass1("rxc", nfull, codes("x", mine), LO, [other["relay"][k]], "uxc")
+        n += pass1("uxc", nlo, codes("x", theirs), FULL, home, "axn")
+        for j in (0, 1):
+            v = T.pf[:, 2 * NC * j:2 * NC * j + 2 * NC]
+            n += pass1("rp%d" % j, nfull, v, LO, [other["fan"][k]], "me%d" % j)
+        n += maker(0, me["port"][k], "rp0", nfull, nlo, "ahq")
+        n += maker(1, mine, "rp1", nfull, nlo, "ahi")
         g.wait_ge(S.loct, n)
         return
     if core in me["fan"]:
         k = me["fan"].index(core)
-        n = 0
-        for t in "xh":
-            n += passon(t, "r", other["port"][k], nlo, FULL, home, "a%sp" % t, "a%sp" % t)
+        n = pass1("rxs", nlo, plane("x", other["port"][k]), FULL, home, "axp")
+        n += pass1("rxc", nlo, codes("x", other["port"][k]), FULL, home, "axp")
+        n += pass1("uxs", nlo, plane("x", other["inner"][k]), FULL, home, "axn")
+        n += maker(0, other["port"][k], "me0", nlo, nhi, "ahp")
+        n += maker(1, other["inner"][k], "me1", nlo, nhi, "ahn")
         g.wait_ge(S.loct, n)
         return
     if core not in home:
@@ -127,16 +179,14 @@ def rank_program(g, core, T, topo):
     lr = home.index(core)
     isport = core in me["port"]
     k = me["port" if isport else "inner"].index(core)
-    mate = other["inner" if isport else "port"][k]
-    owner = {}
-    for kind, by in (("inner", "port"), ("port", "inner")):
-        for c, o in zip(other[kind], me[by]):
-            owner[c] = o
+    owns = {}
+    for c, p in zip(me["inner"], me["port"]):
+        owns[c] = [p, c]
+    owns[me["port"][0]], owns[me["port"][1]] = other["port"], other["inner"]
     tcol = {}
-    for c in home:
-        tcol[c] = 2 * NC * home.index(c)
-    for c in away:
-        tcol[c] = 2 * NC * home.index(owner[c]) + NC
+    for o in home:
+        for j, c in enumerate(owns[o]):
+            tcol[c] = NC * (2 * home.index(o) + j)
     a0, a1 = cols([core])
     w0 = 2 * NC * lr
     ps = T.ps
@@ -149,16 +199,6 @@ def rank_program(g, core, T, topo):
     sy.dma_start(T.w1in[:], T.w1[:]).then_inc(S.lw1, 16)
     sy.wait_ge(S.lx, 16)
     sy.dma_start(T.w2in[:], T.w2[:]).then_inc(S.lw2, 16)
-
-    def gather(t, hh, loc):
-        mask, helper = (LO, other["fan"][k]) if isport else (tosend[t], me["relay"][k])
-        pieces = ((T[t + "s"][:, a0:a1], S["r%ss" % t]), (cv(T[t + "c"], a0, a1), S["r%sc" % t]))
-        n = 0
-        for src, hs in pieces:
-            n += send([(mask, [helper], hs, src, src)], loc)
-        for src, hs in pieces:
-            n += send([(FULL, peers, hh, src, src)], loc)
-        return n
 
     def exchange(owners):
         n = 0
@@ -173,37 +213,59 @@ def rank_program(g, core, T, topo):
                     mv.append((m, [o], sem, cv(T.tc, ta, ta + 2 * NC), cv(T.rc, w0, w0 + 2 * NC)))
                 else:
                     mv.append((m, [o], sem, T.ts[:, ta:ta + 2 * NC], T.rs[:, w0:w0 + 2 * NC]))
-            n += send(mv, S.loct)
+            if mv:
+                n += send(mv, S.loct)
         return n
     qt_home = ((S.qto, 1), (S.qti, len(ipeers)), (S.qtq, len(qpeers)))
     g.wait_ge(S.qx, 1)
-    nl = gather("x", S.axq if isport else S.axi, S.loct)
+    mp, mc, helper = (LO, LO, other["fan"][k]) if isport else (EVEN, FULL, me["relay"][k])
+    nl = 0
+    for v, sem, mask in ((plane("x", core), S.rxs, mp), (codes("x", core), S.rxc, mc)):
+        nl += send([(mask, [helper], sem, v, v)], S.loct)
+    for v in (plane("x", core), codes("x", core)):
+        nl += send([(FULL, peers, S.axq if isport else S.axi, v, v)], S.loct)
     g.wait_ge(S.qw2, 1)
     for src in (cv(T.w2c, w0, w0 + 2 * NC), T.w2s[:, w0:w0 + 2 * NC]):
         nl += send([(FULL, peers, S.aw2, src, src)], S.loct)
     for sem, v in qt_home:
         g.wait_ge(sem, v)
-    g.wait_ge(S.qtp, 2)
     nl += exchange(me["inner"])
-    g.wait_ge(S.qtn, 2)
-    nl += exchange(me["port"])
-    nlp = 0
-    for i in (0, 1):
-        v, w = T.pf[:, NC * i:NC * i + NC], T.pin[:, NC * i:NC * i + NC]
-        g.wait_ge(S["pf%d" % i], 1)
+    g.wait_ge(S.qtp, 1)
+    nl += exchange(me["port"][:1])
+    g.wait_ge(S.qtn, 1)
+    nl += exchange(me["port"][1:])
+    nlp = [0, 0]
+    for j in (0, 1):
+        v = T.pf[:, 2 * NC * j:2 * NC * j + 2 * NC]
+        loc = S["locp%d" % j]
+        g.wait_ge(S["pf%d" % j], 2)
         if isport:
-            nlp += send([(LO, [mate], S["apin%d" % i], v, w)], S.locp)
+            w = T.pin[:, 2 * NC * k:2 * NC * k + 2 * NC]
+            nlp[j] = send([(LO, [other["relay"][j]], S["ml%d" % k], v, w), (HI, [me["fan"][j]], S["ml%d" % k], v, w)], loc)
         else:
-            nlp += send([(FULL, [me["relay"][k]], S["rp%d" % i], v, w)], S.locp)
-    g.wait_ge(S.qh, 1)
-    nlh = gather("h", S.ahq if isport else S.ahi, S.loch)
-    g.wait_ge(S.loch, nlh)
+            nlp[j] = send([(FULL, [me["relay"][k]], S["rp%d" % j], v, v)], loc)
 
     te = g.tensor
 
-    def mm(b, wc, ws, w, mc, ms, a, n, st=True, sp=True):
-        return te.matmul_mx(bank(b, n), wc[:, w:w + NC], ws[:, w:w + NC], mc[:, a:a + n], ms[:, a:a + n], st, sp)
+    def mm(b, wc, ws, w, m_c, m_s, a, n, st=True, sp=True):
+        return te.matmul_mx(bank(b, n), wc[:, w:w + NC], ws[:, w:w + NC], m_c[:, a:a + n], m_s[:, a:a + n], st, sp)
     both = 2 * nfull
+
+    def term(q, c):
+        r = home.index(c)
+        if q:
+            te.wait_ge(S["at%d" % r], 2 * nev if c in me["port"] and not isport else both)
+        else:
+            te.wait_ge(S.qw2, 1)
+            te.wait_ge(S.aw2, 3 * both)
+            late = () if not isport else ((S.qtp, 1),) if k == 0 else ((S.qtn, 1),)
+            for sem, v in qt_home + late:
+                te.wait_ge(sem, v)
+        m_c, m_s = (T.rc, T.rs) if q else (T.tc, T.ts)
+        for i in (0, 1):
+            ins = mm(4 + i, T.w2c, T.w2s, 2 * NC * r + NC * i, m_c, m_s, 2 * NC * r, 2 * NC, q == 0, q == 3)
+            if q == 3:
+                ins.then_inc(S["sum%d" % i], 1)
     groups = (("o", [core], 0, ()),
               ("i", ipeers, 2, ((S.axi, both * len(ipeers)),)),
               ("q", qpeers, 4, ((S.axq, both * len(qpeers)),)),
@@ -212,49 +274,33 @@ def rank_program(g, core, T, topo):
     te.wait_ge(S.qw1, 1)
     te.wait_ge(S.qx, 1)
     for tag, grp, b, waits in groups:
+        if tag == "n" and not isport:
+            term(0, core)
         for sem, v in waits:
             te.wait_ge(sem, v)
         ga, gb = cols(grp)
         for i in (0, 1):
             mm(b + i, T.w1c, T.w1s, NC * i, T.xc, T.xs, ga, gb - ga).then_inc(S["z%s%d" % (tag, i)], 1)
-    te.wait_ge(S.qw2, 1)
-    te.wait_ge(S.aw2, 3 * both)
-    for sem, v in qt_home + ((S.qtp, 2), (S.qtn, 2)):
-        te.wait_ge(sem, v)
     for q, c in enumerate([core] + ipeers + qpeers):
-        r = home.index(c)
-        if q:
-            te.wait_ge(S["at%d" % r], both if (c in me["port"]) == isport else 2 * nev)
-        mc, ms = (T.rc, T.rs) if q else (T.tc, T.ts)
-        for b, off, tag in ((6, NC, "f"), (4, 0, "h")):
-            for i in (0, 1):
-                ins = mm(b + i, T.w2c, T.w2s, 2 * NC * r + NC * i, mc, ms, 2 * NC * r + off, NC, q == 0, q == 3)
-                if q == 3:
-                    ins.then_inc(S["sum%s%d" % (tag, i)], 1)
-    ypairs = ((me["inner"], 0), (me["port"], 2), (other["port"], 6), (other["inner"], 4))
+        if q or isport:
+            term(q, c)
+    ypairs = ((me["port"], 2), (other["port"], 6), (me["inner"], 0), (other["inner"], 4))
+    own = ((S.qh0, 1),)
     before = (
-        ((S.ahi, both * len(ipeers)), (S.asn, 2), (S.avn, 2)),
-        ((S.ahq, both * len(qpeers)), (S.asi, 2), (S.avi, 2)),
-        ((S.ahp, both * 2), (S.pf0, 1), (S.pf1, 1)),
-        ((S.ahn, both * 2), (S.ad0, 1), (S.ad1, 1)))
+        ((S.ahq, both * len(qpeers)),) + own * isport,
+        ((S.ahp, both * 2),),
+        ((S.ahi, both * len(ipeers)),) + own * (not isport),
+        ((S.ahn, both * 2), (S.pf0, 2), (S.pf1, 2)))
     te.wait_ge(S.qw3, 1)
-    te.wait_ge(S.qh, 1)
+    te.wait_ge(S.qtp, 1)
+    te.wait_ge(S.qtn, 1)
     for p, (grp, b) in enumerate(ypairs):
         for sem, v in before[p]:
             te.wait_ge(sem, v)
         g0 = cols(grp)[0]
         for i in (0, 1):
-            mm(b + i, T.w3c, T.w3s, NC * i, T.hc, T.hs, g0, 256).then_inc(S["ly%d%d" % (p, i)], 1)
+            mm(b + i, T.w3c, T.w3s, NC * i, T.hc, T.hs, g0, 2 * NC).then_inc(S["ly%d%d" % (p, i)], 1)
 
-    sc, ve = g.scalar, g.vector
-
-    def act_s(src, n, out, c0, c, sem):
-        for q, sg in ((0, 1.0), (1, -1.0)):
-            sc.activation(out[:, 4 * c0 + q:4 * c0 + 4 * n:4], src, AF.Relu, scale=sg * c).then_inc(sem, 1)
-
-    def act_v(src, n, out, c0, c, sem):
-        for q, sg in ((2, 1.0), (3, -1.0)):
-            ve.tensor_scalar(out[:, 4 * c0 + q:4 * c0 + 4 * n:4], src, sg * c, 0.0, AluOpType.mult, AluOpType.max).then_inc(sem, 1)
     ve.wait_ge(S.lx, 16)
     ve.quantize_mx(T.xc[:, a0:a1], T.xs[:, a0:a1], T.xin[:]).then_inc(S.qx, 1)
     ve.wait_ge(S.lw1, 16)
@@ -262,36 +308,31 @@ def rank_program(g, core, T, topo):
     for tag, grp, b, waits in groups:
         c0, n = cols(grp)[0], NC * len(grp)
         sc.wait_ge(S["z%s0" % tag], 1)
-        act_s(bank(b, n), n, T.tt, c0, C1, S["as" + tag])
         ve.wait_ge(S["z%s1" % tag], 1)
-        act_v(bank(b + 1, n), n, T.tt, c0, C1, S["av" + tag])
+        for q in range(4):
+            act(ve if q // 2 else sc, bank(b + q // 2, n), n, T.tt, c0, C1, q, S[("av" if q // 2 else "as") + tag])
         ve.wait_ge(S["av" + tag], 2)
         ve.wait_ge(S["as" + tag], 2)
-        for c in grp:
+        for c, m in [(grp[0], n)] if tag in "pn" else [(c, NC) for c in grp]:
             u, v = 4 * NC * slot[c], tcol[c]
-            ve.quantize_mx(T.tc[:, v:v + NC], T.ts[:, v:v + NC], T.tt[:, u:u + 4 * NC]).then_inc(S["qt" + tag], 1)
+            ve.quantize_mx(T.tc[:, v:v + m], T.ts[:, v:v + m], T.tt[:, u:u + 4 * m]).then_inc(S["qt" + tag], 1)
         if tag == "o":
             ve.wait_ge(S.lw2, 16)
             ve.quantize_mx(T.w2c[:, w0:w0 + 2 * NC], T.w2s[:, w0:w0 + 2 * NC], T.w2in[:]).then_inc(S.qw2, 1)
-    sc.wait_ge(S.sumf0, 1)
-    sc.activation(T.pf[:, 0:NC], bank(6, NC), AF.Copy).then_inc(S.pf0, 1)
-    ve.wait_ge(S.sumf1, 1)
-    ve.tensor_copy(T.pf[:, NC:2 * NC], bank(7, NC)).then_inc(S.pf1, 1)
+    sc.wait_ge(S.sum0, 1)
+    ve.wait_ge(S.sum1, 1)
+    for j in (0, 1):
+        o = 2 * NC * j
+        sc.activation(T.pf[:, o:o + NC], bank(4, NC, NC * j), AF.Copy).then_inc(S["pf%d" % j], 1)
+        ve.tensor_copy(T.pf[:, o + NC:o + 2 * NC], bank(5, NC, NC * j)).then_inc(S["pf%d" % j], 1)
     ve.wait_ge(S.lw3, 16)
     ve.quantize_mx(T.w3c[:], T.w3s[:], T.w3in[:]).then_inc(S.qw3, 1)
-    for i in (0, 1):
-        ve.wait_ge(S["sumh%d" % i], 1)
-        ve.wait_ge(S["apin%d" % i], nlo)
-        ve.tensor_tensor(T.sf[:, NC * i:NC * i + NC], bank(4 + i, NC), T.pin[:, NC * i:NC * i + NC],
-                         AluOpType.add).then_inc(S["ad%d" % i], 1)
-    sc.wait_ge(S.ad0, 1)
-    act_s(T.sf[:, 0:NC], NC, T.hb, 0, C2, S.hs0)
-    ve.wait_ge(S.ad1, 1)
-    act_v(T.sf[:, NC:2 * NC], NC, T.hb, 0, C2, S.hv0)
-    ve.wait_ge(S.hs0, 2)
-    ve.wait_ge(S.hv0, 2)
-    ve.quantize_mx(T.hc[:, a0:a1], T.hs[:, a0:a1], T.hb[:]).then_inc(S.qh, 1)
+    mine_at = 0 if isport else 1
     for p, (grp, b) in enumerate(ypairs):
+        if p == mine_at:
+            sc.wait_ge(S.full, nfull)
+            ve.wait_ge(S.full, nfull)
+            make_h(None, T.sp, core, 0, S.qh0)
         sc.wait_ge(S["ly%d0" % p], 1)
         ve.wait_ge(S["ly%d1" % p], 1)
         g0 = cols(grp)[0]
@@ -309,18 +350,25 @@ def rank_program(g, core, T, topo):
     def tstore(cs):
         for c in cs:
             store(T.t[slot[c]], T.tt[:, 4 * NC * slot[c]:4 * NC * slot[c] + 4 * NC])
-    for sem, v in qt_home:
+    for sem, v in qt_home + ((S.qtp, 1), (S.qtn, 1)):
         sy.wait_ge(sem, v)
-    tstore(home)
+    nfirst = 0
+    if isport and k:
+        nfirst = 2
+        sy.wait_ge(S.loct, nl)
+        sy.dma_start(T.w3in[:], T.w3[:]).then_inc(S.lw3, 16)
+        tstore(home[:nfirst])
+        sy.wait_ge(S.locp0, nlp[0])
+    else:
+        sy.wait_ge(S.locp0, nlp[0])
+        sy.dma_start(T.w3in[:], T.w3[:]).then_inc(S.lw3, 16)
+    tstore((home + away)[nfirst:])
     sy.wait_ge(S.loct, nl)
-    sy.dma_start(T.w3in[:], T.w3[:]).then_inc(S.lw3, 16)
-    sy.wait_ge(S.locp, nlp)
-    sy.wait_ge(S.qtp, 2)
-    sy.wait_ge(S.qtn, 2)
-    tstore(away)
-    sy.wait_ge(S.loch, nlh)
-    store(T.h[:], T.hb[:])
+    sy.wait_ge(S.locp1, nlp[1])
     for p, (grp, b) in enumerate(ypairs):
+        if p == mine_at:
+            sy.wait_ge(S.qh0, 1)
+            store(T.h[:], T.hb[:, 0:4 * NC])
         sy.wait_ge(S["yc%d" % p], 4)
         g0, g1 = cols(grp)
         store(T.y[:, 2 * g0:2 * g1], T.yb[:, 2 * g0:2 * g1])

from concourse.bass import DstId, RemoteDMATransfer
from concourse.mybir import dt, AluOpType, ActivationFunctionType as AF

NC = 128
C1, C2 = 0.041, 0.0145

BFT, CODES, F32 = "bfloat16", "float8_e4m3fn_x4", "float32"
SCRATCH = {
    "xin": ("sbuf", [128, 512], BFT),
    "tt": ("sbuf", [128, 4096], BFT),
    "hb": ("sbuf", [128, 1024], BFT),
    "pf": ("sbuf", [128, 512], F32),
    "pin": ("sbuf", [128, 512], F32),
    "sf": ("sbuf", [128, 512], F32),
    "sp": ("sbuf", [128, 256], F32),
    "yb": ("sbuf", [128, 2048], F32),
    "ps": ("psum", [128, 4096], F32),
}
for _w in ("w1in", "w2in", "w3in"):
    SCRATCH[_w] = ("sbuf", [128, 1024], BFT)
for _n, _c in (("x", 1024), ("h", 1024), ("w1", 256), ("w2", 1024), ("w3", 256), ("t", 1024), ("r", 1024)):
    SCRATCH[_n + "c"] = ("sbuf", [128, _c], CODES)
    SCRATCH[_n + "s"] = ("sbuf", [128, _c], "uint8")
GROUPS = "oiqpn"
SEMAPHORES = (
    ["lx", "lw1", "lw2", "lw3", "st"]
    + ["qx", "qw1", "qw2", "qw3", "qh0", "qh1"] + ["qt" + a for a in GROUPS]
    + ["z%s%d" % (a, i) for a in GROUPS for i in range(2)]
    + ["a%s%s" % (e, a) for a in GROUPS for e in "sv"]
    + ["sum0", "sum1", "pf0", "pf1"]
    + ["ad%d%d" % (j, i) for j in range(2) for i in range(2)]
    + ["hs0", "hv0", "hs1", "hv1"]
    + ["axi", "axq", "axp", "axn", "aw2", "full", "ahi", "ahq", "ahp", "ahn"]
    + ["at%d" % r for r in range(4)]
    + ["rxc", "rxs", "uxc", "uxs"]
    + ["rp0", "rp1", "me0", "me1", "ml0", "ml1"]
    + ["ly%d%d" % (p, i) for p in range(4) for i in range(2)]
    + ["yc%d" % p for p in range(4)]
    + ["loct", "locp0", "locp1"])


def bits(m):
    return [b for b in range(16) if m >> b & 1]


def setof(bs):
    return sum(1 << b for b in bs)


def plan(T, topo):
    cores = list(T.cores)
    P = {}
    for ch in sorted(set(topo.chip(c) for c in cores)):
        home = [c for c in cores if topo.chip(c) == ch]
        away = [c for c in cores if topo.chip(c) != ch]
        port = [c for c in home if topo.may_write(c, away[0])]
        helpers = [c for c in range(128) if topo.chip(c) == ch and c not in cores]
        relay = [c for c in helpers if topo.may_write(c, away[0])]
        P[ch] = dict(home=home, away=away, port=port, inner=[c for c in home if c not in port],
                     relay=relay, fan=[c for c in helpers if c not in relay])
    return P


def rank_program(g, core, T, topo):
    S = T.sem
    P = plan(T, topo)
    ch = topo.chip(core)
    if ch not in P:
        return
    me = P[ch]
    other = P[[k for k in P if k != ch][0]]
    home, away = me["home"], me["away"]
    slot = {c: i for i, c in enumerate(T.cores)}
    FULL = topo.mask(home[0], home[1])
    LO = topo.mask(me["port"][0], away[0])
    HI = FULL & ~LO
    EVEN, ODD = setof(bits(FULL)[0::2]), setof(bits(FULL)[1::2])
    nfull, nlo, nhi, nev = len(bits(FULL)), len(bits(LO)), len(bits(HI)), len(bits(EVEN))

    def did(c):
        a = topo.addr(c)
        return DstId(rid=a[0], pnc=a[1])

    def send(moves, loc):
        g.remote_dma_fused([RemoteDMATransfer(dst_ids=[did(c) for c in ds], dma_engine_mask=m, remote_sem=rs, srcs=[src],
                                              dsts=[dst] * len(ds)) for m, ds, rs, src, dst in moves], local_sem=loc)
        return sum(len(bits(m)) for m, ds, rs, src, dst in moves)

    def cv(buf, a, b):
        return buf[:, a:b].bitcast(dt.uint8)

    def cols(cs):
        a = NC * min(slot[c] for c in cs)
        return a, a + NC * len(cs)

    def plane(t, rank):
        a, b = cols([rank])
        return T[t + "s"][:, a:b]

    def codes(t, rank):
        a, b = cols([rank])
        return cv(T[t + "c"], a, b)

    def pass1(sem, need, v, mask, ds, to):
        g.wait_ge(S[sem], need)
        return send([(mask, ds, S[to], v, v)], S.loct)

    sc, ve = g.scalar, g.vector

    def act(eng, src, n, out, c0, c, q, sem):
        o = out[:, 4 * c0 + q:4 * c0 + 4 * n:4]
        sg = -c if q % 2 else c
        if eng is sc:
            sc.activation(o, src, AF.Relu, scale=sg).then_inc(sem, 1)
        else:
            ve.tensor_scalar(o, src, sg, 0.0, AluOpType.mult, AluOpType.max).then_inc(sem, 1)

    def make_h(terms, full, rank, j, done):
        ns = 2
        if terms:
            ns = 3
            for i in (0, 1):
                ve.tensor_tensor(full[:, NC * i:NC * i + NC], terms[i][0], terms[i][1], AluOpType.add).then_inc(S["ad%d%d" % (j, i)], 1)
            sc.wait_ge(S["ad%d0" % j], 1)
            ve.wait_ge(S["ad%d1" % j], 1)
        for q in range(4):
            if q == 2 and terms:
                sc.wait_ge(S["ad%d1" % j], 1)
            act(sc if q < ns else ve, full[:, NC * (q // 2):NC * (q // 2) + NC], NC, T.hb, NC * j, C2, q,
                S["hs%d" % j] if q < ns else S["hv%d" % j])
        ve.wait_ge(S["hs%d" % j], ns)
        ve.wait_ge(S["hv%d" % j], 4 - ns)
        a, b = cols([rank])
        ve.quantize_mx(T.hc[:, a:b], T.hs[:, a:b], T.hb[:, 4 * NC * j:4 * NC * j + 4 * NC]).then_inc(done, 1)

    def maker(j, rank, early, need, late, to):
        o = 2 * NC * j
        ve.wait_ge(S[early], need)
        ve.wait_ge(S["ml%d" % j], late)
        sums = T.sf[:, o:o + 2 * NC]
        make_h([(T.pf[:, o + NC * i:o + NC * i + NC], T.pin[:, o + NC * i:o + NC * i + NC]) for i in (0, 1)], sums, rank, j, S["qh%d" % j])
        n = 0
        if rank in home:
            for i in (0, 1):
                g.wait_ge(S["ad%d%d" % (j, i)], 1)
            n += send([(FULL, [rank], S.full, sums, T.sp[:])], S.loct)
        g.wait_ge(S["qh%d" % j], 1)
        for v in (plane("h", rank), codes("h", rank)):
            n += send([(FULL, [c for c in home if c != rank], S[to], v, v)], S.loct)
        return n

    if core in me["relay"]:
        k = me["relay"].index(core)
        mine, theirs = me["inner"][k], other["inner"][k]
        n = pass1("rxs", nev, plane("x", mine), LO, [other["fan"][k]], "uxs")
        n += pass1("rxc", nfull, codes("x", mine), LO, [other["relay"][k]], "uxc")
        n += pass1("uxc", nlo, codes("x", theirs), FULL, home, "axn")
        for j in (0, 1):
            v = T.pf[:, 2 * NC * j:2 * NC * j + 2 * NC]
            n += pass1("rp%d" % j, nfull, v, LO, [other["fan"][k]], "me%d" % j)
        n += maker(0, me["port"][k], "rp0", nfull, nlo, "ahq")
        n += maker(1, mine, "rp1", nfull, nlo, "ahi")
        g.wait_ge(S.loct, n)
        return
    if core in me["fan"]:
        k = me["fan"].index(core)
        n = pass1("rxs", nlo, plane("x", other["port"][k]), FULL, home, "axp")
        n += pass1("rxc", nlo, codes("x", other["port"][k]), FULL, home, "axp")
        n += pass1("uxs", nlo, plane("x", other["inner"][k]), FULL, home, "axn")
        n += maker(0, other["port"][k], "me0", nlo, nhi, "ahp")
        n += maker(1, other["inner"][k], "me1", nlo, nhi, "ahn")
        g.wait_ge(S.loct, n)
        return
    if core not in home:
        return

    peers = [c for c in home if c != core]
    ipeers, qpeers = [c for c in me["inner"] if c != core], [c for c in me["port"] if c != core]
    lr = home.index(core)
    isport = core in me["port"]
    k = me["port" if isport else "inner"].index(core)
    owns = {}
    for c, p in zip(me["inner"], me["port"]):
        owns[c] = [p, c]
    owns[me["port"][0]], owns[me["port"][1]] = other["port"], other["inner"]
    tcol = {}
    for o in home:
        for j, c in enumerate(owns[o]):
            tcol[c] = NC * (2 * home.index(o) + j)
    a0, a1 = cols([core])
    w0 = 2 * NC * lr
    ps = T.ps

    def bank(b, n, a=0):
        return ps[:, 512 * b + a:512 * b + a + n]

    sy = g.sync
    sy.dma_start(T.xin[:], T.x[:]).then_inc(S.lx, 16)
    sy.dma_start(T.w1in[:], T.w1[:]).then_inc(S.lw1, 16)
    sy.wait_ge(S.lx, 16)
    sy.dma_start(T.w2in[:], T.w2[:]).then_inc(S.lw2, 16)

    def exchange(owners):
        n = 0
        ds = [o for o in owners if o != core]
        masks = [FULL] if len(ds) == 1 else [EVEN, ODD]
        sem = S["at%d" % lr]
        for cod in (1, 0):
            mv = []
            for m, o in zip(masks, ds):
                ta = 2 * NC * home.index(o)
                if cod:
                    mv.append((m, [o], sem, cv(T.tc, ta, ta + 2 * NC), cv(T.rc, w0, w0 + 2 * NC)))
                else:
                    mv.append((m, [o], sem, T.ts[:, ta:ta + 2 * NC], T.rs[:, w0:w0 + 2 * NC]))
            if mv:
                n += send(mv, S.loct)
        return n
    qt_home = ((S.qto, 1), (S.qti, len(ipeers)), (S.qtq, len(qpeers)))
    g.wait_ge(S.qx, 1)
    mp, mc, helper = (LO, LO, other["fan"][k]) if isport else (EVEN, FULL, me["relay"][k])
    nl = 0
    for v, sem, mask in ((plane("x", core), S.rxs, mp), (codes("x", core), S.rxc, mc)):
        nl += send([(mask, [helper], sem, v, v)], S.loct)
    for v in (plane("x", core), codes("x", core)):
        nl += send([(FULL, peers, S.axq if isport else S.axi, v, v)], S.loct)
    g.wait_ge(S.qw2, 1)
    for src in (cv(T.w2c, w0, w0 + 2 * NC), T.w2s[:, w0:w0 + 2 * NC]):
        nl += send([(FULL, peers, S.aw2, src, src)], S.loct)
    for sem, v in qt_home:
        g.wait_ge(sem, v)
    nl += exchange(me["inner"])
    g.wait_ge(S.qtp, 1)
    nl += exchange(me["port"][:1])
    g.wait_ge(S.qtn, 1)
    nl += exchange(me["port"][1:])
    nlp = [0, 0]
    for j in (0, 1):
        v = T.pf[:, 2 * NC * j:2 * NC * j + 2 * NC]
        loc = S["locp%d" % j]
        g.wait_ge(S["pf%d" % j], 2)
        if isport:
            w = T.pin[:, 2 * NC * k:2 * NC * k + 2 * NC]
            nlp[j] = send([(LO, [other["relay"][j]], S["ml%d" % k], v, w), (HI, [me["fan"][j]], S["ml%d" % k], v, w)], loc)
        else:
            nlp[j] = send([(FULL, [me["relay"][k]], S["rp%d" % j], v, v)], loc)

    te = g.tensor

    def mm(b, wc, ws, w, m_c, m_s, a, n, st=True, sp=True):
        return te.matmul_mx(bank(b, n), wc[:, w:w + NC], ws[:, w:w + NC], m_c[:, a:a + n], m_s[:, a:a + n], st, sp)
    both = 2 * nfull

    def term(q, c):
        r = home.index(c)
        if q:
            te.wait_ge(S["at%d" % r], 2 * nev if c in me["port"] and not isport else both)
        else:
            te.wait_ge(S.qw2, 1)
            te.wait_ge(S.aw2, 3 * both)
            late = () if not isport else ((S.qtp, 1),) if k == 0 else ((S.qtn, 1),)
            for sem, v in qt_home + late:
                te.wait_ge(sem, v)
        m_c, m_s = (T.rc, T.rs) if q else (T.tc, T.ts)
        for i in (0, 1):
            ins = mm(4 + i, T.w2c, T.w2s, 2 * NC * r + NC * i, m_c, m_s, 2 * NC * r, 2 * NC, q == 0, q == 3)
            if q == 3:
                ins.then_inc(S["sum%d" % i], 1)
    groups = (("o", [core], 0, ()),
              ("i", ipeers, 2, ((S.axi, both * len(ipeers)),)),
              ("q", qpeers, 4, ((S.axq, both * len(qpeers)),)),
              ("p", other["port"], 6, ((S.axp, both * 2),)),
              ("n", other["inner"], 0, ((S.axn, both * 2), (S.aso, 2), (S.avo, 2))))
    te.wait_ge(S.qw1, 1)
    te.wait_ge(S.qx, 1)
    for tag, grp, b, waits in groups:
        if tag == "n" and not isport:
            term(0, core)
        for sem, v in waits:
            te.wait_ge(sem, v)
        ga, gb = cols(grp)
        for i in (0, 1):
            mm(b + i, T.w1c, T.w1s, NC * i, T.xc, T.xs, ga, gb - ga).then_inc(S["z%s%d" % (tag, i)], 1)
    for q, c in enumerate([core] + ipeers + qpeers):
        if q or isport:
            term(q, c)
    ypairs = ((me["port"], 2), (other["port"], 6), (me["inner"], 0), (other["inner"], 4))
    own = ((S.qh0, 1),)
    before = (
        ((S.ahq, both * len(qpeers)),) + own * isport,
        ((S.ahp, both * 2),),
        ((S.ahi, both * len(ipeers)),) + own * (not isport),
        ((S.ahn, both * 2), (S.pf0, 2), (S.pf1, 2)))
    te.wait_ge(S.qw3, 1)
    te.wait_ge(S.qtp, 1)
    te.wait_ge(S.qtn, 1)
    for p, (grp, b) in enumerate(ypairs):
        for sem, v in before[p]:
            te.wait_ge(sem, v)
        g0 = cols(grp)[0]
        for i in (0, 1):
            mm(b + i, T.w3c, T.w3s, NC * i, T.hc, T.hs, g0, 2 * NC).then_inc(S["ly%d%d" % (p, i)], 1)

    ve.wait_ge(S.lx, 16)
    ve.quantize_mx(T.xc[:, a0:a1], T.xs[:, a0:a1], T.xin[:]).then_inc(S.qx, 1)
    ve.wait_ge(S.lw1, 16)
    ve.quantize_mx(T.w1c[:], T.w1s[:], T.w1in[:]).then_inc(S.qw1, 1)
    for tag, grp, b, waits in groups:
        c0, n = cols(grp)[0], NC * len(grp)
        sc.wait_ge(S["z%s0" % tag], 1)
        ve.wait_ge(S["z%s1" % tag], 1)
        for q in range(4):
            act(ve if q // 2 else sc, bank(b + q // 2, n), n, T.tt, c0, C1, q, S[("av" if q // 2 else "as") + tag])
        ve.wait_ge(S["av" + tag], 2)
        ve.wait_ge(S["as" + tag], 2)
        for c, m in [(grp[0], n)] if tag in "pn" else [(c, NC) for c in grp]:
            u, v = 4 * NC * slot[c], tcol[c]
            ve.quantize_mx(T.tc[:, v:v + m], T.ts[:, v:v + m], T.tt[:, u:u + 4 * m]).then_inc(S["qt" + tag], 1)
        if tag == "o":
            ve.wait_ge(S.lw2, 16)
            ve.quantize_mx(T.w2c[:, w0:w0 + 2 * NC], T.w2s[:, w0:w0 + 2 * NC], T.w2in[:]).then_inc(S.qw2, 1)
    sc.wait_ge(S.sum0, 1)
    ve.wait_ge(S.sum1, 1)
    for j in (0, 1):
        o = 2 * NC * j
        sc.activation(T.pf[:, o:o + NC], bank(4, NC, NC * j), AF.Copy).then_inc(S["pf%d" % j], 1)
        ve.tensor_copy(T.pf[:, o + NC:o + 2 * NC], bank(5, NC, NC * j)).then_inc(S["pf%d" % j], 1)
    ve.wait_ge(S.lw3, 16)
    ve.quantize_mx(T.w3c[:], T.w3s[:], T.w3in[:]).then_inc(S.qw3, 1)
    mine_at = 0 if isport else 1
    for p, (grp, b) in enumerate(ypairs):
        if p == mine_at:
            sc.wait_ge(S.full, nfull)
            ve.wait_ge(S.full, nfull)
            make_h(None, T.sp, core, 0, S.qh0)
        sc.wait_ge(S["ly%d0" % p], 1)
        ve.wait_ge(S["ly%d1" % p], 1)
        g0 = cols(grp)[0]
        for q in (0, 1):
            o = 2 * (g0 + NC * q)
            sc.activation(T.yb[:, o:o + NC], bank(b, NC, NC * q), AF.Copy).then_inc(S["yc%d" % p], 1)
            ve.tensor_copy(T.yb[:, o + NC:o + 2 * NC], bank(b + 1, NC, NC * q)).then_inc(S["yc%d" % p], 1)

    nst = [0]

    def store(out, in_):
        sy.dma_start(out, in_).then_inc(S.st, 16)
        nst[0] += 16

    def tstore(cs):
        for c in cs:
            store(T.t[slot[c]], T.tt[:, 4 * NC * slot[c]:4 * NC * slot[c] + 4 * NC])
    for sem, v in qt_home + ((S.qtp, 1), (S.qtn, 1)):
        sy.wait_ge(sem, v)
    nfirst = 0
    if isport and k:
        nfirst = 2
        sy.wait_ge(S.loct, nl)
        sy.dma_start(T.w3in[:], T.w3[:]).then_inc(S.lw3, 16)
        tstore(home[:nfirst])
        sy.wait_ge(S.locp0, nlp[0])
    else:
        sy.wait_ge(S.locp0, nlp[0])
        sy.dma_start(T.w3in[:], T.w3[:]).then_inc(S.lw3, 16)
    tstore((home + away)[nfirst:])
    sy.wait_ge(S.loct, nl)
    sy.wait_ge(S.locp1, nlp[1])
    for p, (grp, b) in enumerate(ypairs):
        if p == mine_at:
            sy.wait_ge(S.qh0, 1)
            store(T.h[:], T.hb[:, 0:4 * NC])
        sy.wait_ge(S["yc%d" % p], 4)
        g0, g1 = cols(grp)
        store(T.y[:, 2 * g0:2 * g1], T.yb[:, 2 * g0:2 * g1])
    sy.wait_ge(S.st, nst[0])
